import numpy as np, ml_dtypes
CORES = [129,145,193,257,273,321,385,401,449]
N = 9
KB, QP = 2, 64
MEM = [2,5]
def setup_inputs(rng):
    q = rng.standard_normal((N, 128, QP), dtype=np.float32) / 4; k = rng.standard_normal((N, 128, KB * 128), dtype=np.float32)
    a = 2 * np.pi * rng.random((N, QP)); s = 400 * rng.random((N, QP)) ** 1.5; q[:, 0, :] = s * np.cos(a); q[:, 1, :] = s * np.sin(a); q[:, 2, :] = 150 * rng.standard_normal((N, QP)); k[:, 2, :] = 1 + k[:, 2, :] / 50
    c = np.zeros(N); c[MEM] = rng.permutation(len(MEM))
    a = (2 * np.pi * rng.random() + np.pi / 2 * (c.reshape(N, 1, 1) + 0.5) / len(MEM) - 0.5 + (np.arange(KB).reshape(1, KB, 1) + rng.random((N, KB, 128))) / KB).reshape(N, KB * 128); k[:, 0, :] = np.cos(a); k[:, 1, :] = np.sin(a)
    return {"q": q.astype(ml_dtypes.bfloat16), "k": k.astype(ml_dtypes.bfloat16), "v": rng.standard_normal((N, 128, KB * 128), dtype=np.float32).astype(ml_dtypes.bfloat16)}
def setup_inputs_big(rng):
    d = setup_inputs(rng)
    for k in ("v",): d[k] = (d[k].astype(np.float32) * 1048576.0).astype(d[k].dtype)
    return d
def setup_inputs_small(rng):
    d = setup_inputs(rng)
    for k in ("v",): d[k] = (d[k].astype(np.float32) * (1 / 1048576.0)).astype(d[k].dtype)
    return d
def reference(q, k, v):
    Q, K, V = q.astype(np.float64), k.astype(np.float64), v.astype(np.float64)
    y = np.zeros((N, QP, 128))
    for r in range(N):
        js = list(MEM)
        S = np.concatenate([K[j].T @ Q[r] for j in js], axis=0)
        P = np.exp(S - S.max(axis=0)); P = P / P.sum(axis=0)
        y[r] = P.T @ np.concatenate([V[j][:, 128 * b:128 * b + 128] for j in js for b in range(KB)], axis=0)
    return {"y": y.astype(ml_dtypes.bfloat16)}

@@ -1,0 +1,273 @@
+from concourse.bass import DstId, RemoteDMATransfer
+from concourse.mybir import AluOpType, AxisListType, ActivationFunctionType
+
+QP = 64
+KW = 256
+NT = 3
+
+SCRATCH = {
+    "Kb": ("sbuf", [128, 2 * KW], "bfloat16"),
+    "Vb": ("sbuf", [128, 2 * KW], "bfloat16"),
+    "Qa": ("sbuf", [128, 128 * (NT - 1) + QP], "bfloat16"),
+    "ident": ("sbuf", [128, 128], "bfloat16"),
+    "P": ("sbuf", [128, NT * 2 * KW], "bfloat16"),
+    "PT": ("sbuf", [128, NT * 2 * KW], "bfloat16"),
+    "Oo": ("sbuf", [128, NT * 128], "bfloat16"),
+    "Da": ("sbuf", [128, NT * 128], "bfloat16"),
+    "Ys": ("sbuf", [128, NT * 128], "bfloat16"),
+    "st": ("sbuf", [128, NT * 8], "float32"),
+    "A0": ("psum", [128, 512], "float32"), "A1": ("psum", [128, 512], "float32"), "A2": ("psum", [128, 512], "float32"),
+    "T0": ("psum", [128, 1024], "bfloat16"), "T1": ("psum", [128, 1024], "bfloat16"), "T2": ("psum", [128, 1024], "bfloat16"),
+    "Y0": ("psum", [128, 512], "float32"), "Y1": ("psum", [128, 512], "float32"),
+}
+_STAGES = ["o1", "o2", "o3", "o4", "o5", "o6", "o7", "x1", "x2a", "x2", "x3", "x3p", "x4a", "x4b", "x4c", "x5", "x6",
+           "x7", "x8"]
+SEMAPHORES = (["kl", "vl", "ql", "ka", "va", "qa0", "qa1", "ya", "ls", "sd", "ms", "mz", "idn"]
+              + ["%s_%d" % (s, t) for t in range(NT) for s in _STAGES])
+
+
+def _plan(T, topo):
+    cores, hubs = list(T.cores), list(T.tables["MEM"])
+    rest = [r for r in range(len(cores)) if r not in hubs]
+    cap = -(-len(rest) // len(hubs))
+    cl = {h: [] for h in hubs}
+    free = []
+    for r in rest:
+        c = [h for h in hubs if topo.may_write(cores[r], cores[h]) and topo.may_write(cores[h], cores[r])]
+        if len(c) == 1:
+            cl[c[0]].append(r)
+        else:
+            free.append((r, c))
+    for r, c in free:
+        rk = topo.rack(topo.host(cores[r]))
+        order = sorted(c, key=lambda h: topo.rack(topo.host(cores[h])) != rk)
+        room = [h for h in order if len(cl[h]) < cap]
+        cl[(room or order)[0]].append(r)
+    return {h: [sorted(cl[h])[i:i + 2] for i in range(0, len(cl[h]), 2)] + [[h]] for h in hubs}
+
+
+def _bits(mask):
+    return bin(mask).count("1")
+
+
+def _leaf(g, core, T, topo, hub_core, tile, pos):
+    sem = T.sem
+    g.sync.dma_start(T.Qa[:, 0:QP], T.q[:]).then_inc(sem.ql, 16)
+    rid, pid = topo.addr(hub_core, core)
+    m = topo.mask(core, hub_core)
+    c0 = 128 * tile + QP * pos
+    g.wait_ge(sem.ql, 16)
+    g.remote_dma(T.Qa[:, c0:c0 + QP], T.Qa[:, 0:QP], sem["qa%d" % tile], sem.ls, pid, rid, m)
+    g.sync.wait_ge(sem.ya, _bits(topo.mask(hub_core, core)))
+    g.sync.dma_start(T.y[:], T.Ys[QP * pos:QP * pos + QP, 0:128]).then_inc(sem.sd, 16)
+    g.sync.wait_ge(sem.sd, 16)
+    g.wait_ge(sem.ls, _bits(m))
+
+
+def _hub(g, core, T, topo, other_core, tiles):
+    sem, cores = T.sem, list(T.cores)
+    PE, DVE, ACT = g.tensor, g.vector, g.scalar
+    Exp, Copy = ActivationFunctionType.Exp, ActivationFunctionType.Copy
+    W = len(tiles) - 1
+    seen = {}
+
+    def wait(q, name, n):
+        k = (q, name)
+        if seen.get(k, 0) < n:
+            seen[k] = n
+            {"pe": PE, "dve": DVE, "act": ACT, "g": g, "sync": g.sync}[q].wait_ge(sem[name], n)
+
+    def s(t, st):
+        return "%s_%d" % (st, t)
+
+    M = [QP * len(tl) for tl in tiles]
+    A = [T["A%d" % t] for t in range(NT)]
+    TT = [T["T%d" % t] for t in range(NT)]
+
+    def q_of(t):
+        return T.Qa[:, 128 * t:128 * t + M[t]]
+
+    def col(t, i):
+        return T.st[0:M[t], 8 * t + i:8 * t + i + 1]
+
+    def ps_o(t):
+        return A[t][0:M[t], 0:128] if t == W else T["Y%d" % t][0:M[t], 0:128]
+
+    def ps_y(t):
+        return A[t][0:M[t], 128:256] if t == W else T["Y%d" % t][0:M[t], 128:256]
+
+    g.sync.dma_start(T.Kb[:, 0:KW], T.k[:]).then_inc(sem.kl, 16)
+    g.scalar.dma_start(q_of(W), T.q[:]).then_inc(sem.ql, 16)
+    g.sync.dma_start(T.Vb[:, 0:KW], T.v[:]).then_inc(sem.vl, 16)
+    DVE.memset(T.ident[:], 1.0).then_inc(sem.ms, 1)
+    lone = [t for t in range(W) if M[t] < 128]
+    for t in lone:
+        DVE.memset(T.Ys[M[t]:128, 128 * t:128 * t + 128], 0.0).then_inc(sem.mz, 1)
+    wait("g", "ms", 1)
+    g.affine_select(T.ident[:], T.ident[:], [[-1, 128]], AluOpType.is_equal, 0.0, 0, 1).then_inc(sem.idn, 1)
+    rid, pid = topo.addr(other_core, core)
+    mo = topo.mask(core, other_core)
+    ne = _bits(mo)
+    sent = 0
+    wait("g", "kl", 16)
+    g.remote_dma(T.Kb[:, KW:2 * KW], T.Kb[:, 0:KW], sem.ka, sem.ls, pid, rid, mo)
+    wait("g", "vl", 16)
+    g.remote_dma(T.Vb[:, KW:2 * KW], T.Vb[:, 0:KW], sem.va, sem.ls, pid, rid, mo)
+    sent += 2 * ne
+
+    def scores(t, h):
+        if h == 0:
+            wait("pe", "kl", 16)
+            if t == W:
+                wait("pe", "ql", 16)
+            else:
+                wait("pe", "qa%d" % t, sum(_bits(topo.mask(cores[r], core)) for r in tiles[t]))
+        else:
+            wait("pe", "ka", _bits(topo.mask(other_core, core)))
+            if t == W:
+                wait("pe", s(t, "o7"), 1)
+        PE.matmul(A[t][0:M[t], KW * h:KW * h + KW], q_of(t), T.Kb[:, KW * h:KW * h + KW], True, True) \
+            .then_inc(sem[s(t, "x1" if h else "o1")], 1)
+
+    def negmax(t, h):
+        wait("dve", s(t, "x1" if h else "o1"), 1)
+        DVE.tensor_reduce(col(t, h), A[t][0:M[t], KW * h:KW * h + KW], AxisListType.X, AluOpType.max, negate=True) \
+            .then_inc(sem[s(t, "x2a" if h else "o2")], 1)
+        if h:
+            wait("dve", s(t, "x2a"), 1)
+            wait("dve", s(t, "o2"), 1)
+            DVE.tensor_tensor(col(t, 2), col(t, 0), col(t, 1), AluOpType.min).then_inc(sem[s(t, "x2")], 1)
+
+    def weights(t, h):
+        wait("act", s(t, "x1" if h else "o1"), 1)
+        wait("act", s(t, "x2" if h else "o2"), 1)
+        p0 = 2 * KW * t + KW * h
+        ACT.activation(T.P[0:M[t], p0:p0 + KW], A[t][0:M[t], KW * h:KW * h + KW], Exp, bias=col(t, 2 * h), scale=1.0,
+                       accum_out=col(t, 3 + h)).then_inc(sem[s(t, "x3" if h else "o3")], 1)
+        if h:
+            wait("act", s(t, "o2"), 1)
+            ACT.activation(col(t, 5), col(t, 0), Exp, bias=col(t, 2), scale=-1.0).then_inc(sem[s(t, "x3p")], 1)
+
+    def turn(t, h):
+        wait("pe", s(t, "x3" if h else "o3"), 1)
+        wait("pe", "idn", 1)
+        p0 = 2 * KW * t + KW * h
+        for b in range(2):
+            PE.transpose(TT[t][:, KW * h + b * M[t]:KW * h + (b + 1) * M[t]], T.P[0:M[t], p0 + 128 * b:p0 + 128 * b + 128],
+                         T.ident[0:M[t], 0:M[t]]).then_inc(sem[s(t, "x5" if h else "o4")], 1)
+
+    def turned(t, h):
+        wait("dve", s(t, "x5" if h else "o4"), 2)
+        p0 = 2 * KW * t + KW * h
+        DVE.tensor_copy(T.PT[:, p0:p0 + 2 * M[t]], TT[t][:, KW * h:KW * h + 2 * M[t]]) \
+            .then_inc(sem[s(t, "x6" if h else "o5")], 1)
+
+    def pv(t, h):
+        wait("pe", s(t, "x6" if h else "o5"), 1)
+        if h:
+            wait("pe", "va", _bits(topo.mask(other_core, core)))
+        else:
+            wait("pe", "vl", 16)
+        p0 = 2 * KW * t + KW * h
+        for b in range(2):
+            i = PE.matmul(ps_y(t) if h else ps_o(t), T.PT[:, p0 + b * M[t]:p0 + (b + 1) * M[t]],
+                          T.Vb[:, KW * h + 128 * b:KW * h + 128 * b + 128], (not h) and b == 0, b == 1)
+        i.then_inc(sem[s(t, "x7" if h else "o6")], 1)
+
+    def keep_own(t):
+        wait("act", s(t, "o6"), 1)
+        ACT.activation(T.Oo[0:M[t], 128 * t:128 * t + 128], ps_o(t), Copy).then_inc(sem[s(t, "o7")], 1)
+
+    def diag(t):
+        wait("dve", s(t, "x3p"), 1)
+        wait("dve", "idn", 1)
+        DVE.tensor_scalar(T.Da[0:M[t], 128 * t:128 * t + M[t]], T.ident[0:M[t], 0:M[t]], col(t, 5), None, AluOpType.mult) \
+            .then_inc(sem[s(t, "x4a")], 1)
+
+    def norm(t):
+        wait("dve", s(t, "x3p"), 1)
+        wait("dve", s(t, "x3"), 1)
+        wait("dve", s(t, "o3"), 1)
+        DVE.tensor_scalar(col(t, 6), col(t, 3), col(t, 5), col(t, 4), AluOpType.mult, AluOpType.add) \
+            .then_inc(sem[s(t, "x4b")], 1)
+        wait("dve", s(t, "x4b"), 1)
+        DVE.reciprocal(col(t, 7), col(t, 6)).then_inc(sem[s(t, "x4c")], 1)
+
+    def merge(t):
+        wait("pe", s(t, "x4a"), 1)
+        wait("pe", s(t, "o7"), 1)
+        PE.matmul(ps_y(t), T.Da[0:M[t], 128 * t:128 * t + M[t]], T.Oo[0:M[t], 128 * t:128 * t + 128], True, False)
+
+    def finish(t):
+        wait("act", s(t, "x7"), 1)
+        wait("act", s(t, "x4c"), 1)
+        ACT.activation(T.Ys[0:M[t], 128 * t:128 * t + 128], ps_y(t), Copy, scale=col(t, 7)).then_inc(sem[s(t, "x8")], 1)
+
+    C = list(range(W))
+    for f in (scores, negmax, weights, turn, turned, pv):
+        f(W, 0)
+    keep_own(W)
+    for f in (scores, negmax, weights, turn, turned, pv):
+        for t in C:
+            f(t, 0)
+    for t in C:
+        keep_own(t)
+    for t in C + [W]:
+        scores(t, 1)
+    for t in C:
+        negmax(t, 1)
+    for t in C:
+        weights(t, 1)
+    for i, t in enumerate(C):
+        turn(t, 1)
+        if i:
+            pv(C[i - 1], 1)
+        diag(t)
+        merge(t)
+        turned(t, 1)
+        norm(t)
+    pv(C[-1], 1)
+    for t in C:
+        finish(t)
+        wait("g", s(t, "x8"), 1)
+        if t in lone:
+            wait("g", "mz", len(lone))
+        src = T.Ys[:, 128 * t:128 * t + 128]
+        dst = [cores[r] for r in tiles[t]]
+        m = topo.mask(core, dst[0])
+        for d in dst:
+            m &= topo.mask(core, d)
+        ids = [topo.addr(d, core) for d in dst]
+        g.remote_dma_fused([RemoteDMATransfer(dst_ids=[DstId(rid=a, pnc=b) for a, b in ids], dma_engine_mask=m,
+                                              remote_sem=sem.ya, srcs=[src], dsts=[T.Ys[:, 0:128] for d in dst])],
+                           local_sem=sem.ls)
+        sent += _bits(m)
+    negmax(W, 1)
+    weights(W, 1)
+    turn(W, 1)
+    diag(W)
+    merge(W)
+    turned(W, 1)
+    norm(W)
+    pv(W, 1)
+    finish(W)
+    wait("sync", s(W, "x8"), 1)
+    g.sync.dma_start(T.y[:], T.Ys[0:QP, 128 * W:128 * W + 128]).then_inc(sem.sd, 16)
+    g.sync.wait_ge(sem.sd, 16)
+    g.wait_ge(sem.ls, sent)
+
+
+def rank_program(g, core, T, topo):
+    rank = T.rank_of(core)
+    if rank is None:
+        return
+    plan = _plan(T, topo)
+    cores = list(T.cores)
+    if rank in plan:
+        other = [h for h in plan if h != rank][0]
+        _hub(g, core, T, topo, cores[other], plan[rank])
+        return
+    for h, tiles in plan.items():
+        for t, tl in enumerate(tiles):
+            if rank in tl:
+                _leaf(g, core, T, topo, cores[h], t, tl.index(rank))

@@ -14,7 +14,9 @@ SCRATCH = {
     "PT": ("sbuf", [128, NT * 2 * KW], "bfloat16"),
     "Oo": ("sbuf", [128, NT * 128], "bfloat16"),
     "Da": ("sbuf", [128, NT * 128], "bfloat16"),
-    "Ys": ("sbuf", [128, NT * 128], "bfloat16"),
+    "Ys": ("sbuf", [128, 128], "bfloat16"),
+    "Yr": ("sbuf", [128, 2 * (NT - 1) * QP], "bfloat16"),
+    "Yl": ("sbuf", [128, QP], "bfloat16"),
     "st": ("sbuf", [128, NT * 8], "float32"),
     "A0": ("psum", [128, 512], "float32"), "A1": ("psum", [128, 512], "float32"), "A2": ("psum", [128, 512], "float32"),
     "T0": ("psum", [128, 1024], "bfloat16"), "T1": ("psum", [128, 1024], "bfloat16"), "T2": ("psum", [128, 1024], "bfloat16"),
@@ -22,7 +24,7 @@ SCRATCH = {
 }
 _STAGES = ["o1", "o2", "o3", "o4", "o5", "o6", "o7", "x1", "x2a", "x2", "x3", "x3p", "x4a", "x4b", "x4c", "x5", "x6",
            "x7", "x8"]
-SEMAPHORES = (["kl", "vl", "ql", "ka", "va", "qa0", "qa1", "ya", "ls", "sd", "ms", "mz", "idn"]
+SEMAPHORES = (["kl", "vl", "ql", "ka", "va", "qa0", "qa1", "ya", "ls", "sd", "ms", "idn"]
               + ["%s_%d" % (s, t) for t in range(NT) for s in _STAGES])
 
 
@@ -50,7 +52,16 @@ def _bits(mask):
     return bin(mask).count("1")
 
 
-def _leaf(g, core, T, topo, hub_core, tile, pos):
+def _ymasks(topo, hub_core, dst):
+    m = topo.mask(hub_core, dst[0])
+    for d in dst:
+        m &= topo.mask(hub_core, d)
+    e = [1 << i for i in range(m.bit_length()) if (m >> i) & 1]
+    per = len(e) // len(dst)
+    return [sum(e[i * per:(i + 1) * per]) for i in range(len(dst))]
+
+
+def _leaf(g, core, T, topo, hub_core, tile, pos, tile_cores):
     sem = T.sem
     g.sync.dma_start(T.Qa[:, 0:QP], T.q[:]).then_inc(sem.ql, 16)
     rid, pid = topo.addr(hub_core, core)
@@ -58,9 +69,12 @@ def _leaf(g, core, T, topo, hub_core, tile, pos):
     c0 = 128 * tile + QP * pos
     g.wait_ge(sem.ql, 16)
     g.remote_dma(T.Qa[:, c0:c0 + QP], T.Qa[:, 0:QP], sem["qa%d" % tile], sem.ls, pid, rid, m)
-    g.sync.wait_ge(sem.ya, _bits(topo.mask(hub_core, core)))
-    g.sync.dma_start(T.y[:], T.Ys[QP * pos:QP * pos + QP, 0:128]).then_inc(sem.sd, 16)
-    g.sync.wait_ge(sem.sd, 16)
+    n = _bits(_ymasks(topo, hub_core, tile_cores)[pos])
+    g.sync.wait_ge(sem.ya, n)
+    g.sync.dma_start(T.y[:, 0:QP], T.Yl[0:QP, :]).then_inc(sem.sd, 16)
+    g.scalar.wait_ge(sem.ya, n)
+    g.scalar.dma_start(T.y[:, QP:2 * QP], T.Yl[QP:2 * QP, :]).then_inc(sem.sd, 16)
+    g.sync.wait_ge(sem.sd, 32)
     g.wait_ge(sem.ls, _bits(m))
 
 
@@ -100,9 +114,6 @@ def _hub(g, core, T, topo, other_core, tiles):
     g.scalar.dma_start(q_of(W), T.q[:]).then_inc(sem.ql, 16)
     g.sync.dma_start(T.Vb[:, 0:KW], T.v[:]).then_inc(sem.vl, 16)
     DVE.memset(T.ident[:], 1.0).then_inc(sem.ms, 1)
-    lone = [t for t in range(W) if M[t] < 128]
-    for t in lone:
-        DVE.memset(T.Ys[M[t]:128, 128 * t:128 * t + 128], 0.0).then_inc(sem.mz, 1)
     wait("g", "ms", 1)
     g.affine_select(T.ident[:], T.ident[:], [[-1, 128]], AluOpType.is_equal, 0.0, 0, 1).then_inc(sem.idn, 1)
     rid, pid = topo.addr(other_core, core)
@@ -198,50 +209,95 @@ def _hub(g, core, T, topo, other_core, tiles):
         wait("pe", s(t, "o7"), 1)
         PE.matmul(ps_y(t), T.Da[0:M[t], 128 * t:128 * t + M[t]], T.Oo[0:M[t], 128 * t:128 * t + 128], True, False)
 
+    def max1(t):
+        wait("dve", s(t, "o1"), 1)
+        wait("dve", s(t, "x1"), 1)
+        DVE.tensor_reduce(col(t, 2), A[t][0:M[t], 0:2 * KW], AxisListType.X, AluOpType.max, negate=True) \
+            .then_inc(sem[s(t, "x2")], 1)
+
+    def exp1(t, h):
+        wait("act", s(t, "o1"), 1)
+        wait("act", s(t, "x1"), 1)
+        wait("act", s(t, "x2"), 1)
+        p0 = 2 * KW * t + KW * h
+        ACT.activation(T.P[0:M[t], p0:p0 + KW], A[t][0:M[t], KW * h:KW * h + KW], Exp, bias=col(t, 2), scale=1.0,
+                       accum_out=col(t, 3 + h)).then_inc(sem[s(t, "x3" if h else "o3")], 1)
+
+    def turn1(t):
+        wait("pe", "idn", 1)
+        for h in range(2):
+            wait("pe", s(t, "x3" if h else "o3"), 1)
+            for j in (2 * h, 2 * h + 1):
+                PE.transpose(TT[t][:, j * M[t]:(j + 1) * M[t]],
+                             T.P[0:M[t], 2 * KW * t + 128 * j:2 * KW * t + 128 * j + 128],
+                             T.ident[0:M[t], 0:M[t]]).then_inc(sem[s(t, "x5")], 1)
+
+    def turned1(t):
+        wait("dve", s(t, "x5"), 4)
+        DVE.tensor_copy(T.PT[:, 2 * KW * t:2 * KW * t + 4 * M[t]], TT[t][:, 0:4 * M[t]]).then_inc(sem[s(t, "x6")], 1)
+
+    def norm1(t):
+        wait("dve", s(t, "o3"), 1)
+        wait("dve", s(t, "x3"), 1)
+        DVE.tensor_tensor(col(t, 6), col(t, 3), col(t, 4), AluOpType.add).then_inc(sem[s(t, "x4b")], 1)
+        wait("dve", s(t, "x4b"), 1)
+        DVE.reciprocal(col(t, 7), col(t, 6)).then_inc(sem[s(t, "x4c")], 1)
+
+    def pv1(t):
+        wait("pe", s(t, "x6"), 1)
+        wait("pe", "vl", 16)
+        wait("pe", "va", _bits(topo.mask(other_core, core)))
+        for j in range(4):
+            i = PE.matmul(ps_y(t), T.PT[:, 2 * KW * t + j * M[t]:2 * KW * t + (j + 1) * M[t]],
+                          T.Vb[:, 128 * j:128 * j + 128], j == 0, j == 3)
+        i.then_inc(sem[s(t, "x7")], 1)
+
+    def slot(t, p):
+        return T.Yr[:, QP * (2 * t + p):QP * (2 * t + p) + QP]
+
     def finish(t):
         wait("act", s(t, "x7"), 1)
         wait("act", s(t, "x4c"), 1)
-        ACT.activation(T.Ys[0:M[t], 128 * t:128 * t + 128], ps_y(t), Copy, scale=col(t, 7)).then_inc(sem[s(t, "x8")], 1)
+        if t == W:
+            ACT.activation(T.Ys[0:M[t], 0:128], ps_y(t), Copy, scale=col(t, 7)).then_inc(sem[s(t, "x8")], 1)
+            return
+        for p in range(len(tiles[t])):
+            c0 = QP * (2 * t + p)
+            for h in range(2):
+                ACT.activation(T.Yr[QP * h:QP * h + QP, c0:c0 + QP],
+                               T["Y%d" % t][QP * p:QP * p + QP, 128 + QP * h:128 + QP * h + QP], Copy,
+                               scale=T.st[QP * p:QP * p + QP, 8 * t + 7:8 * t + 8]).then_inc(sem[s(t, "x8")], 1)
 
     C = list(range(W))
     for f in (scores, negmax, weights, turn, turned, pv):
         f(W, 0)
     keep_own(W)
-    for f in (scores, negmax, weights, turn, turned, pv):
-        for t in C:
-            f(t, 0)
     for t in C:
-        keep_own(t)
-    for t in C + [W]:
+        scores(t, 0)
         scores(t, 1)
+    scores(W, 1)
     for t in C:
-        negmax(t, 1)
+        max1(t)
     for t in C:
-        weights(t, 1)
-    for i, t in enumerate(C):
-        turn(t, 1)
-        if i:
-            pv(C[i - 1], 1)
-        diag(t)
-        merge(t)
-        turned(t, 1)
-        norm(t)
-    pv(C[-1], 1)
+        exp1(t, 0)
+        exp1(t, 1)
+    for t in C:
+        turn1(t)
+    for t in C:
+        norm1(t)
+        turned1(t)
+    for t in C:
+        pv1(t)
     for t in C:
         finish(t)
-        wait("g", s(t, "x8"), 1)
-        if t in lone:
-            wait("g", "mz", len(lone))
-        src = T.Ys[:, 128 * t:128 * t + 128]
+        wait("g", s(t, "x8"), 2 * len(tiles[t]))
         dst = [cores[r] for r in tiles[t]]
-        m = topo.mask(core, dst[0])
-        for d in dst:
-            m &= topo.mask(core, d)
+        ms = _ymasks(topo, core, dst)
         ids = [topo.addr(d, core) for d in dst]
-        g.remote_dma_fused([RemoteDMATransfer(dst_ids=[DstId(rid=a, pnc=b) for a, b in ids], dma_engine_mask=m,
-                                              remote_sem=sem.ya, srcs=[src], dsts=[T.Ys[:, 0:128] for d in dst])],
-                           local_sem=sem.ls)
-        sent += _bits(m)
+        g.remote_dma_fused([RemoteDMATransfer(dst_ids=[DstId(rid=ids[p][0], pnc=ids[p][1])], dma_engine_mask=ms[p],
+                                              remote_sem=sem.ya, srcs=[slot(t, p)], dsts=[T.Yl[:]])
+                            for p in range(len(dst))], local_sem=sem.ls)
+        sent += sum(_bits(x) for x in ms)
     negmax(W, 1)
     weights(W, 1)
     turn(W, 1)
@@ -252,7 +308,7 @@ def _hub(g, core, T, topo, other_core, tiles):
     pv(W, 1)
     finish(W)
     wait("sync", s(W, "x8"), 1)
-    g.sync.dma_start(T.y[:], T.Ys[0:QP, 128 * W:128 * W + 128]).then_inc(sem.sd, 16)
+    g.sync.dma_start(T.y[:], T.Ys[0:QP, 0:128]).then_inc(sem.sd, 16)
     g.sync.wait_ge(sem.sd, 16)
     g.wait_ge(sem.ls, sent)
 
@@ -270,4 +326,4 @@ def rank_program(g, core, T, topo):
     for h, tiles in plan.items():
         for t, tl in enumerate(tiles):
             if rank in tl:
-                _leaf(g, core, T, topo, cores[h], t, tl.index(rank))
+                _leaf(g, core, T, topo, cores[h], t, tl.index(rank), [cores[r] for r in tl])

from concourse.bass import DstId, RemoteDMATransfer
from concourse.mybir import AluOpType, AxisListType, ActivationFunctionType

QP = 64
KW = 256
NT = 3

SCRATCH = {
    "Kb": ("sbuf", [128, 2 * KW], "bfloat16"),
    "Vb": ("sbuf", [128, 2 * KW], "bfloat16"),
    "Qa": ("sbuf", [128, 128 * (NT - 1) + QP], "bfloat16"),
    "ident": ("sbuf", [128, 128], "bfloat16"),
    "P": ("sbuf", [128, NT * 2 * KW], "bfloat16"),
    "PT": ("sbuf", [128, NT * 2 * KW], "bfloat16"),
    "Oo": ("sbuf", [128, NT * 128], "bfloat16"),
    "Da": ("sbuf", [128, NT * 128], "bfloat16"),
    "Ys": ("sbuf", [128, 128], "bfloat16"),
    "Yr": ("sbuf", [128, 2 * (NT - 1) * QP], "bfloat16"),
    "Yl": ("sbuf", [128, QP], "bfloat16"),
    "st": ("sbuf", [128, NT * 8], "float32"),
    "A0": ("psum", [128, 512], "float32"), "A1": ("psum", [128, 512], "float32"), "A2": ("psum", [128, 512], "float32"),
    "T0": ("psum", [128, 1024], "bfloat16"), "T1": ("psum", [128, 1024], "bfloat16"), "T2": ("psum", [128, 1024], "bfloat16"),
    "Y0": ("psum", [128, 512], "float32"), "Y1": ("psum", [128, 512], "float32"),
}
_STAGES = ["o1", "o2", "o3", "o4", "o5", "o6", "o7", "x1", "x2a", "x2", "x3", "x3p", "x4a", "x4b", "x4c", "x5", "x6",
           "x7", "x8"]
SEMAPHORES = (["kl", "vl", "ql", "ka", "va", "qa0", "qa1", "ya", "ls", "sd", "ms", "idn"]
              + ["%s_%d" % (s, t) for t in range(NT) for s in _STAGES])


def _plan(T, topo):
    cores, hubs = list(T.cores), list(T.tables["MEM"])
    rest = [r for r in range(len(cores)) if r not in hubs]
    cap = -(-len(rest) // len(hubs))
    cl = {h: [] for h in hubs}
    free = []
    for r in rest:
        c = [h for h in hubs if topo.may_write(cores[r], cores[h]) and topo.may_write(cores[h], cores[r])]
        if len(c) == 1:
            cl[c[0]].append(r)
        else:
            free.append((r, c))
    for r, c in free:
        rk = topo.rack(topo.host(cores[r]))
        order = sorted(c, key=lambda h: topo.rack(topo.host(cores[h])) != rk)
        room = [h for h in order if len(cl[h]) < cap]
        cl[(room or order)[0]].append(r)
    return {h: [sorted(cl[h])[i:i + 2] for i in range(0, len(cl[h]), 2)] + [[h]] for h in hubs}


def _bits(mask):
    return bin(mask).count("1")


def _ymasks(topo, hub_core, dst):
    m = topo.mask(hub_core, dst[0])
    for d in dst:
        m &= topo.mask(hub_core, d)
    e = [1 << i for i in range(m.bit_length()) if (m >> i) & 1]
    per = len(e) // len(dst)
    return [sum(e[i * per:(i + 1) * per]) for i in range(len(dst))]


def _leaf(g, core, T, topo, hub_core, tile, pos, tile_cores):
    sem = T.sem
    g.sync.dma_start(T.Qa[:, 0:QP], T.q[:]).then_inc(sem.ql, 16)
    rid, pid = topo.addr(hub_core, core)
    m = topo.mask(core, hub_core)
    c0 = 128 * tile + QP * pos
    g.wait_ge(sem.ql, 16)
    g.remote_dma(T.Qa[:, c0:c0 + QP], T.Qa[:, 0:QP], sem["qa%d" % tile], sem.ls, pid, rid, m)
    n = _bits(_ymasks(topo, hub_core, tile_cores)[pos])
    g.sync.wait_ge(sem.ya, n)
    g.sync.dma_start(T.y[:, 0:QP], T.Yl[0:QP, :]).then_inc(sem.sd, 16)
    g.scalar.wait_ge(sem.ya, n)
    g.scalar.dma_start(T.y[:, QP:2 * QP], T.Yl[QP:2 * QP, :]).then_inc(sem.sd, 16)
    g.sync.wait_ge(sem.sd, 32)
    g.wait_ge(sem.ls, _bits(m))


def _hub(g, core, T, topo, other_core, tiles):
    sem, cores = T.sem, list(T.cores)
    PE, DVE, ACT = g.tensor, g.vector, g.scalar
    Exp, Copy = ActivationFunctionType.Exp, ActivationFunctionType.Copy
    W = len(tiles) - 1
    seen = {}

    def wait(q, name, n):
        k = (q, name)
        if seen.get(k, 0) < n:
            seen[k] = n
            {"pe": PE, "dve": DVE, "act": ACT, "g": g, "sync": g.sync}[q].wait_ge(sem[name], n)

    def s(t, st):
        return "%s_%d" % (st, t)

    M = [QP * len(tl) for tl in tiles]
    A = [T["A%d" % t] for t in range(NT)]
    TT = [T["T%d" % t] for t in range(NT)]

    def q_of(t):
        return T.Qa[:, 128 * t:128 * t + M[t]]

    def col(t, i):
        return T.st[0:M[t], 8 * t + i:8 * t + i + 1]

    def ps_o(t):
        return A[t][0:M[t], 0:128] if t == W else T["Y%d" % t][0:M[t], 0:128]

    def ps_y(t):
        return A[t][0:M[t], 128:256] if t == W else T["Y%d" % t][0:M[t], 128:256]

    g.sync.dma_start(T.Kb[:, 0:KW], T.k[:]).then_inc(sem.kl, 16)
    g.scalar.dma_start(q_of(W), T.q[:]).then_inc(sem.ql, 16)
    g.sync.dma_start(T.Vb[:, 0:KW], T.v[:]).then_inc(sem.vl, 16)
    DVE.memset(T.ident[:], 1.0).then_inc(sem.ms, 1)
    wait("g", "ms", 1)
    g.affine_select(T.ident[:], T.ident[:], [[-1, 128]], AluOpType.is_equal, 0.0, 0, 1).then_inc(sem.idn, 1)
    rid, pid = topo.addr(other_core, core)
    mo = topo.mask(core, other_core)
    ne = _bits(mo)
    sent = 0
    wait("g", "kl", 16)
    g.remote_dma(T.Kb[:, KW:2 * KW], T.Kb[:, 0:KW], sem.ka, sem.ls, pid, rid, mo)
    wait("g", "vl", 16)
    g.remote_dma(T.Vb[:, KW:2 * KW], T.Vb[:, 0:KW], sem.va, sem.ls, pid, rid, mo)
    sent += 2 * ne

    def scores(t, h):
        if h == 0:
            wait("pe", "kl", 16)
            if t == W:
                wait("pe", "ql", 16)
            else:
                wait("pe", "qa%d" % t, sum(_bits(topo.mask(cores[r], core)) for r in tiles[t]))
        else:
            wait("pe", "ka", _bits(topo.mask(other_core, core)))
            if t == W:
                wait("pe", s(t, "o7"), 1)
        PE.matmul(A[t][0:M[t], KW * h:KW * h + KW], q_of(t), T.Kb[:, KW * h:KW * h + KW], True, True) \
            .then_inc(sem[s(t, "x1" if h else "o1")], 1)

    def negmax(t, h):
        wait("dve", s(t, "x1" if h else "o1"), 1)
        DVE.tensor_reduce(col(t, h), A[t][0:M[t], KW * h:KW * h + KW], AxisListType.X, AluOpType.max, negate=True) \
            .then_inc(sem[s(t, "x2a" if h else "o2")], 1)
        if h:
            wait("dve", s(t, "x2a"), 1)
            wait("dve", s(t, "o2"), 1)
            DVE.tensor_tensor(col(t, 2), col(t, 0), col(t, 1), AluOpType.min).then_inc(sem[s(t, "x2")], 1)

    def weights(t, h):
        wait("act", s(t, "x1" if h else "o1"), 1)
        wait("act", s(t, "x2" if h else "o2"), 1)
        p0 = 2 * KW * t + KW * h
        ACT.activation(T.P[0:M[t], p0:p0 + KW], A[t][0:M[t], KW * h:KW * h + KW], Exp, bias=col(t, 2 * h), scale=1.0,
                       accum_out=col(t, 3 + h)).then_inc(sem[s(t, "x3" if h else "o3")], 1)
        if h:
            wait("act", s(t, "o2"), 1)
            ACT.activation(col(t, 5), col(t, 0), Exp, bias=col(t, 2), scale=-1.0).then_inc(sem[s(t, "x3p")], 1)

    def turn(t, h):
        wait("pe", s(t, "x3" if h else "o3"), 1)
        wait("pe", "idn", 1)
        p0 = 2 * KW * t + KW * h
        for b in range(2):
            PE.transpose(TT[t][:, KW * h + b * M[t]:KW * h + (b + 1) * M[t]], T.P[0:M[t], p0 + 128 * b:p0 + 128 * b + 128],
                         T.ident[0:M[t], 0:M[t]]).then_inc(sem[s(t, "x5" if h else "o4")], 1)

    def turned(t, h):
        wait("dve", s(t, "x5" if h else "o4"), 2)
        p0 = 2 * KW * t + KW * h
        DVE.tensor_copy(T.PT[:, p0:p0 + 2 * M[t]], TT[t][:, KW * h:KW * h + 2 * M[t]]) \
            .then_inc(sem[s(t, "x6" if h else "o5")], 1)

    def pv(t, h):
        wait("pe", s(t, "x6" if h else "o5"), 1)
        if h:
            wait("pe", "va", _bits(topo.mask(other_core, core)))
        else:
            wait("pe", "vl", 16)
        p0 = 2 * KW * t + KW * h
        for b in range(2):
            i = PE.matmul(ps_y(t) if h else ps_o(t), T.PT[:, p0 + b * M[t]:p0 + (b + 1) * M[t]],
                          T.Vb[:, KW * h + 128 * b:KW * h + 128 * b + 128], (not h) and b == 0, b == 1)
        i.then_inc(sem[s(t, "x7" if h else "o6")], 1)

    def keep_own(t):
        wait("act", s(t, "o6"), 1)
        ACT.activation(T.Oo[0:M[t], 128 * t:128 * t + 128], ps_o(t), Copy).then_inc(sem[s(t, "o7")], 1)

    def diag(t):
        wait("dve", s(t, "x3p"), 1)
        wait("dve", "idn", 1)
        DVE.tensor_scalar(T.Da[0:M[t], 128 * t:128 * t + M[t]], T.ident[0:M[t], 0:M[t]], col(t, 5), None, AluOpType.mult) \
            .then_inc(sem[s(t, "x4a")], 1)

    def norm(t):
        wait("dve", s(t, "x3p"), 1)
        wait("dve", s(t, "x3"), 1)
        wait("dve", s(t, "o3"), 1)
        DVE.tensor_scalar(col(t, 6), col(t, 3), col(t, 5), col(t, 4), AluOpType.mult, AluOpType.add) \
            .then_inc(sem[s(t, "x4b")], 1)
        wait("dve", s(t, "x4b"), 1)
        DVE.reciprocal(col(t, 7), col(t, 6)).then_inc(sem[s(t, "x4c")], 1)

    def merge(t):
        wait("pe", s(t, "x4a"), 1)
        wait("pe", s(t, "o7"), 1)
        PE.matmul(ps_y(t), T.Da[0:M[t], 128 * t:128 * t + M[t]], T.Oo[0:M[t], 128 * t:128 * t + 128], True, False)

    def max1(t):
        wait("dve", s(t, "o1"), 1)
        wait("dve", s(t, "x1"), 1)
        DVE.tensor_reduce(col(t, 2), A[t][0:M[t], 0:2 * KW], AxisListType.X, AluOpType.max, negate=True) \
            .then_inc(sem[s(t, "x2")], 1)

    def exp1(t, h):
        wait("act", s(t, "o1"), 1)
        wait("act", s(t, "x1"), 1)
        wait("act", s(t, "x2"), 1)
        p0 = 2 * KW * t + KW * h
        ACT.activation(T.P[0:M[t], p0:p0 + KW], A[t][0:M[t], KW * h:KW * h + KW], Exp, bias=col(t, 2), scale=1.0,
                       accum_out=col(t, 3 + h)).then_inc(sem[s(t, "x3" if h else "o3")], 1)

    def turn1(t):
        wait("pe", "idn", 1)
        for h in range(2):
            wait("pe", s(t, "x3" if h else "o3"), 1)
            for j in (2 * h, 2 * h + 1):
                PE.transpose(TT[t][:, j * M[t]:(j + 1) * M[t]],
                             T.P[0:M[t], 2 * KW * t + 128 * j:2 * KW * t + 128 * j + 128],
                             T.ident[0:M[t], 0:M[t]]).then_inc(sem[s(t, "x5")], 1)

    def turned1(t):
        wait("dve", s(t, "x5"), 4)
        DVE.tensor_copy(T.PT[:, 2 * KW * t:2 * KW * t + 4 * M[t]], TT[t][:, 0:4 * M[t]]).then_inc(sem[s(t, "x6")], 1)

    def norm1(t):
        wait("dve", s(t, "o3"), 1)
        wait("dve", s(t, "x3"), 1)
        DVE.tensor_tensor(col(t, 6), col(t, 3), col(t, 4), AluOpType.add).then_inc(sem[s(t, "x4b")], 1)
        wait("dve", s(t, "x4b"), 1)
        DVE.reciprocal(col(t, 7), col(t, 6)).then_inc(sem[s(t, "x4c")], 1)

    def pv1(t):
        wait("pe", s(t, "x6"), 1)
        wait("pe", "vl", 16)
        wait("pe", "va", _bits(topo.mask(other_core, core)))
        for j in range(4):
            i = PE.matmul(ps_y(t), T.PT[:, 2 * KW * t + j * M[t]:2 * KW * t + (j + 1) * M[t]],
                          T.Vb[:, 128 * j:128 * j + 128], j == 0, j == 3)
        i.then_inc(sem[s(t, "x7")], 1)

    def slot(t, p):
        return T.Yr[:, QP * (2 * t + p):QP * (2 * t + p) + QP]

    def finish(t):
        wait("act", s(t, "x7"), 1)
        wait("act", s(t, "x4c"), 1)
        if t == W:
            ACT.activation(T.Ys[0:M[t], 0:128], ps_y(t), Copy, scale=col(t, 7)).then_inc(sem[s(t, "x8")], 1)
            return
        for p in range(len(tiles[t])):
            c0 = QP * (2 * t + p)
            for h in range(2):
                ACT.activation(T.Yr[QP * h:QP * h + QP, c0:c0 + QP],
                               T["Y%d" % t][QP * p:QP * p + QP, 128 + QP * h:128 + QP * h + QP], Copy,
                               scale=T.st[QP * p:QP * p + QP, 8 * t + 7:8 * t + 8]).then_inc(sem[s(t, "x8")], 1)

    C = list(range(W))
    for f in (scores, negmax, weights, turn, turned, pv):
        f(W, 0)
    keep_own(W)
    for t in C:
        scores(t, 0)
        scores(t, 1)
    scores(W, 1)
    for t in C:
        max1(t)
    for t in C:
        exp1(t, 0)
        exp1(t, 1)
    for t in C:
        turn1(t)
    for t in C:
        norm1(t)
        turned1(t)
    for t in C:
        pv1(t)
    for t in C:
        finish(t)
        wait("g", s(t, "x8"), 2 * len(tiles[t]))
        dst = [cores[r] for r in tiles[t]]
        ms = _ymasks(topo, core, dst)
        ids = [topo.addr(d, core) for d in dst]
        g.remote_dma_fused([RemoteDMATransfer(dst_ids=[DstId(rid=ids[p][0], pnc=ids[p][1])], dma_engine_mask=ms[p],
                                              remote_sem=sem.ya, srcs=[slot(t, p)], dsts=[T.Yl[:]])
                            for p in range(len(dst))], local_sem=sem.ls)
        sent += sum(_bits(x) for x in ms)
    negmax(W, 1)
    weights(W, 1)
    turn(W, 1)
    diag(W)
    merge(W)
    turned(W, 1)
    norm(W)
    pv(W, 1)
    finish(W)
    wait("sync", s(W, "x8"), 1)
    g.sync.dma_start(T.y[:], T.Ys[0:QP, 0:128]).then_inc(sem.sd, 16)
    g.sync.wait_ge(sem.sd, 16)
    g.wait_ge(sem.ls, sent)


def rank_program(g, core, T, topo):
    rank = T.rank_of(core)
    if rank is None:
        return
    plan = _plan(T, topo)
    cores = list(T.cores)
    if rank in plan:
        other = [h for h in plan if h != rank][0]
        _hub(g, core, T, topo, cores[other], plan[rank])
        return
    for h, tiles in plan.items():
        for t, tl in enumerate(tiles):
            if rank in tl:
                _leaf(g, core, T, topo, cores[h], t, tl.index(rank), [cores[r] for r in tl])
